import numpy as np
import ml_dtypes


def mxq(x, axis, fmt="e4m3"):
    dtype, down = {"e4m3": (ml_dtypes.float8_e4m3fn, 7), "e5m2": (ml_dtypes.float8_e5m2, 14)}[fmt]
    v = np.moveaxis(np.asarray(x, np.float32).astype(ml_dtypes.bfloat16).astype(np.float64), axis, -1)
    blocks = v.reshape(v.shape[:-1] + (-1, 32))
    amax = np.abs(blocks).max(-1, keepdims=True)
    byte = np.maximum(np.where(amax > 0, np.frexp(amax)[1] - 1 + 127, 0) - down, 1)
    scale = np.exp2(byte - 127.0)
    codes = (blocks / scale).astype(np.float32).astype(dtype).astype(np.float64)
    return np.moveaxis((codes * scale).reshape(v.shape), -1, axis)


WIDE = False


def mx_kscale(k):
    if not WIDE:
        return np.ones(k)
    levels = np.array([10, -10, 5, -5, 0])
    if k % 512:
        return np.exp2(np.random.permutation(np.resize(levels, k // 32))).repeat(32)
    a = np.empty((k // 512, 16))
    for p in range(k // 512):
        a[p, :8] = np.random.permutation(np.resize(levels, 8))
        for g in range(8):
            far = levels[np.abs(levels - a[p, g]) >= 10]
            a[p, g + 8] = far[np.random.randint(len(far))]
    return np.exp2(a.ravel()).repeat(32)


def f64(x):
    return np.asarray(x).astype(np.float64)


def striped(idx):
    return np.tile(idx.reshape(-1, 16).T, (8, 1)).astype(np.uint16)


def unstriped(offs):
    return offs[:16].T.reshape(-1).astype(np.int64)


def striped8(idx):
    return np.concatenate([x.reshape(-1, 16).T for x in idx]).astype(np.uint16)


def runs(offs, k):
    lists = np.stack([offs[16 * r : 16 * r + 16].T.reshape(-1) for r in range(8)]).astype(np.int64)
    return lists[np.arange(k) % 512 // 64]


def pack_weight(w):
    k, n = w.shape
    w = f64(np.asarray(w, np.float32).astype(ml_dtypes.bfloat16)).reshape(k // 32, 32, n)
    amax = np.abs(w).max(1)
    byte = np.clip(np.where(amax > 0, np.frexp(amax)[1] - 1 + 127 - 7, 1), 1, 254)
    scaled = (w * np.exp2(127.0 - byte)[:, None, :]).reshape(k, n).astype(np.float32)
    words = np.ascontiguousarray(scaled.reshape(k // 512, 128, 4, n).transpose(0, 1, 3, 2)).astype(ml_dtypes.float8_e4m3fn).view(np.uint8)
    return words, np.ascontiguousarray(byte.astype(np.uint8).reshape(k // 512, 16, n))


def unpack_weight(words, scales):
    g, p, n, _ = words.shape
    vals = np.ascontiguousarray(words).view(ml_dtypes.float8_e4m3fn).astype(np.float64) * np.repeat(np.exp2(scales.astype(np.float64) - 127.0), 8, axis=1)[..., None]
    return vals.transpose(0, 1, 3, 2).reshape(g * 512, n)


def sigmoid(v):
    return 1.0 / (1.0 + np.exp(-np.maximum(v, -700.0)))


K, T, S, H = 512, 2048, 512, 512


def setup_inputs():
    n = np.random.standard_normal
    s = mx_kscale(K)[:, None]
    u = mx_kscale(S)
    packed_xT = pack_weight(n((K, T)) * s)
    return {
        "x_words": packed_xT[0],
        "x_scales": packed_xT[1],
        "w1": (n((K, H)) / np.sqrt(K) / s).astype(np.float32),
        "ga": (np.random.uniform(0.5, 1.5, (H, 1)) * u[:, None]).astype(np.float32),
        "gb": (np.random.uniform(0.5, 1.5, (H, 1)) / u[:, None]).astype(np.float32),
        "offs": striped(np.random.permutation(T)[:S]),
        "n1": striped8(np.stack([np.random.permutation(S) for _ in range(8)])),
        "n2": striped8(np.stack([np.random.permutation(S) for _ in range(8)])),
        "n3": striped8(np.stack([np.random.permutation(S) for _ in range(8)])),
        "n4": striped8(np.stack([np.random.permutation(S) for _ in range(8)])),
        "n5": striped8(np.stack([np.random.permutation(S) for _ in range(8)])),
    }


def reference(x_words, x_scales, w1, ga, gb, offs, n1, n2, n3, n4, n5):
    xq = unpack_weight(x_words, x_scales)[:, unstriped(offs)]
    y = mxq(f64(w1), 0, "e4m3").T @ xq
    z = f64(ga) * ((y[np.arange(H)[:, None], runs(n1, H)]) * sigmoid(y) + (y[np.arange(H)[:, None], runs(n2, H)]) * (sigmoid(y[np.arange(H)[:, None], runs(n3, H)])))
    z2 = f64(gb) * (y / (np.abs(y[np.arange(H)[:, None], runs(n4, H)]) + 0.5))
    s = 0.0625 * ((mxq(z, 0, "e4m3").T @ mxq(z2, 0, "e4m3")))
    st = s * (sigmoid(s[np.arange(S)[:, None], runs(n5, S)]))
    return np.maximum(st, st[np.arange(S)[:, None], runs(n5, S)])

@@ -1,0 +1,221 @@
+from contextlib import ExitStack
+
+import concourse.mybir as mybir
+
+F32 = mybir.dt.float32
+BF16 = mybir.dt.bfloat16
+I32 = mybir.dt.int32
+U32 = mybir.dt.uint32
+U16 = mybir.dt.uint16
+U8 = mybir.dt.uint8
+FP8X4 = mybir.dt.float8_e4m3fn_x4
+ACT = mybir.ActivationFunctionType
+ALU = mybir.AluOpType
+
+P = 128
+PACK = 4
+T = 2048
+S = 512
+HALF = S // 2
+LIST_HALF = HALF // 16
+TINY = 2.0 ** -60
+
+FLOPS = 2 * 2 * 512 * 512 * 512
+
+
+def tile_picked_selfwsumnormtwicp_none_p_kernel(
+    tc, x_words, x_scales, w1, ga, gb, offs, n1, n2, n3, n4, n5, out
+):
+    nc = tc.nc
+    with ExitStack() as ctx:
+        lists = ctx.enter_context(tc.tile_pool(name="lists", bufs=1))
+        sb = ctx.enter_context(tc.tile_pool(name="sb", bufs=1))
+        psum = ctx.enter_context(tc.psum_pool(name="psum", bufs=1))
+
+        def load_list(name, src):
+            tile = lists.tile([P, S // 16], U16, name=name)
+            nc.sync.dma_start(tile[:], src)
+            return tile
+
+        def cols(h):
+            return slice(h * HALF, (h + 1) * HALF)
+
+        def plane(t, h=None):
+            if h is None:
+                return slice(t * S, (t + 1) * S)
+            return slice(t * S + h * HALF, t * S + (h + 1) * HALF)
+
+        def look_up(window, idx, h):
+            return window[:].indirect(idx[:, h * LIST_HALF : (h + 1) * LIST_HALF])
+
+        xs_all = sb.tile([P, T], U8, name="xs_all")
+        nc.vector.memset(xs_all[:].bitcast(I32), 0)
+        offs_t = load_list("offs_t", offs)
+        for q in range(4):
+            nc.scalar.dma_start(
+                xs_all[32 * q : 32 * q + 4, :].bitcast(I32), x_scales[0, 4 * q : 4 * q + 4, :].bitcast(I32)
+            )
+        xw_all = sb.tile([P, T], I32, name="xw_all")
+        nc.sync.dma_start(xw_all[:], x_words[0].rearrange("p c r -> p (c r)").bitcast(I32))
+        w_rows = w1.rearrange("(p j) c -> p j c", j=PACK)
+        w_raw = []
+        for h in range(2):
+            tile = sb.tile([P, PACK, HALF], F32, name=f"w_raw{h}")
+            nc.sync.dma_start(tile[:], w_rows[:, :, cols(h)])
+            w_raw.append(tile)
+        ga_t = sb.tile([P, PACK], F32, name="ga_t")
+        nc.sync.dma_start(ga_t[:], ga.rearrange("(p t) o -> p (t o)", t=PACK))
+        gb_t = sb.tile([P, PACK], F32, name="gb_t")
+        nc.sync.dma_start(gb_t[:], gb.rearrange("(p t) o -> p (t o)", t=PACK))
+        n1_t = load_list("n1_t", n1)
+        n3_t = load_list("n3_t", n3)
+        n2_t = load_list("n2_t", n2)
+        n4_t = load_list("n4_t", n4)
+        n5_t = load_list("n5_t", n5)
+
+        xs = sb.tile([P, S], U8, name="xs", align_bytes=64)
+        nc.vector.tensor_copy(xs[:], xs_all[:].indirect(offs_t[:]))
+        xw = sb.tile([P, S], U32, name="xw", align_bytes=64)
+        nc.vector.tensor_copy(xw[:], xw_all[:].bitcast(U32).indirect(offs_t[:]))
+
+        w_bf = sb.tile([P, PACK * S], BF16, name="w_bf", align_bytes=64)
+        w_dst = w_bf[:].rearrange("p (t h m j) -> p h m j t", t=PACK, h=2, j=PACK)
+        nc.scalar.copy(w_dst[:, 0], w_raw[0][:].rearrange("p j (m t) -> p m j t", t=PACK))
+        nc.vector.tensor_copy(w_dst[:, 1], w_raw[1][:].rearrange("p j (m t) -> p m j t", t=PACK))
+        w_codes = sb.tile([P, S], U32, name="w_codes", align_bytes=64)
+        w_scales = sb.tile([P, S], U8, name="w_scales", align_bytes=64)
+        y_ps = []
+        for t in range(PACK):
+            m_cols = slice(t * P, (t + 1) * P)
+            nc.vector.quantize_mx(out=w_codes[:, m_cols].bitcast(FP8X4), scales=w_scales[:, m_cols], in_=w_bf[:, plane(t)])
+            bank = psum.tile([P, S], F32, name=f"y_ps{t}")
+            nc.tensor.matmul_mx(
+                out=bank[:], lhsT=w_codes[:, m_cols].bitcast(FP8X4), lhsT_scale=w_scales[:, m_cols],
+                rhs=xw[:].bitcast(FP8X4), rhs_scale=xs[:], start=True, stop=True,
+            )
+            y_ps.append(bank)
+
+        y = [sb.tile([P, S], F32, name=f"y{t}") for t in range(PACK)]
+        ln2y = [sb.tile([P, S], F32, name=f"ln2y{t}") for t in range(PACK)]
+        y_abs = sb.tile([P, PACK * S], F32, name="y_abs", tag="act")
+        for t in range(PACK):
+            if t % 2 == 0:
+                nc.scalar.activation(y_abs[:, plane(t)], y_ps[t][:], ACT.Abs)
+            else:
+                nc.vector.tensor_copy(y[t][:], y_ps[t][:])
+                nc.vector.scalar_tensor_tensor(y_abs[:, plane(t)], y_ps[t][:], -1.0, y[t][:], ALU.mult, ALU.max)
+            nc.scalar.activation(ln2y[t][:], y_abs[:, plane(t)], ACT.Ln, bias=TINY, scale=2.0)
+        for t in range(0, PACK, 2):
+            nc.vector.tensor_copy(y[t][:], y_ps[t][:])
+        y_ga = [sb.tile([P, S], F32, name=f"y_ga{t}") for t in range(PACK)]
+        y_gb = sb.tile([P, PACK * S], F32, name="y_gb")
+        for t in range(PACK):
+            nc.vector.tensor_scalar(y_ga[t][:], y[t][:], ga_t[:, t : t + 1], None, ALU.mult)
+        for t in range(PACK):
+            nc.vector.tensor_scalar(y_gb[:, plane(t)], y[t][:], gb_t[:, t : t + 1], 2.0, ALU.mult, ALU.mult)
+
+        sig = sb.tile([P, 3 * PACK * S], F32, name="sig", tag="act")
+        sig_y = sig[:, 0 : PACK * S]
+        sig_n3 = sig[:, PACK * S : 2 * PACK * S]
+        inv = sig[:, 2 * PACK * S : 3 * PACK * S]
+        prod1 = sb.tile([P, PACK * S], F32, name="prod1")
+        prod2 = sb.tile([P, PACK * S], F32, name="prod2")
+        for t in range(PACK):
+            nc.scalar.activation(sig_y[:, plane(t)], y[t][:], ACT.Sigmoid)
+            for h in range(2):
+                nc.scalar.activation(sig_n3[:, plane(t, h)], look_up(y[t], n3_t, h), ACT.Sigmoid)
+            for h in range(2):
+                nc.vector.tensor_tensor(prod1[:, plane(t, h)], look_up(y_ga[t], n1_t, h), sig_y[:, plane(t, h)], ALU.mult)
+            for h in range(2):
+                nc.vector.tensor_tensor(prod2[:, plane(t, h)], look_up(y_ga[t], n2_t, h), sig_n3[:, plane(t, h)], ALU.mult)
+        for h in range(2):
+            for t in range(PACK):
+                lo = (h * PACK + t) * HALF
+                nc.scalar.activation(inv[:, lo : lo + HALF], look_up(ln2y[t], n4_t, h), ACT.Sigmoid, scale=-1.0)
+
+        z_codes = [sb.tile([P, 2 * P], U32, name=f"z_codes{u}", align_bytes=64) for u in range(2)]
+        z_scales = [sb.tile([P, 2 * P], U8, name=f"z_scales{u}", align_bytes=64) for u in range(2)]
+        z2_codes = sb.tile([P, S], U32, name="z2_codes", align_bytes=64)
+        z2_scales = sb.tile([P, S], U8, name="z2_scales", align_bytes=64)
+        z_bf = [sb.tile([P, 2 * S], BF16, name=f"z_bf{u}", align_bytes=64) for u in range(2)]
+        z2_bf = [sb.tile([P, 2 * S], BF16, name=f"z2_bf{h}", align_bytes=64) for h in range(2)]
+        s_ps = [psum.tile([P, S], F32, name=f"s_ps{t}") for t in range(PACK)]
+        s = [sb.tile([P, S], F32, name=f"s{t}") for t in range(PACK)]
+
+        def z_sum(u):
+            pattern = "p (t m u v) -> p u m t v"
+            nc.vector.tensor_tensor(
+                z_bf[u][:].rearrange("p (v m t) -> p m t v", v=2, t=PACK),
+                prod1[:].rearrange(pattern, t=PACK, u=2, v=2)[:, u],
+                prod2[:].rearrange(pattern, t=PACK, u=2, v=2)[:, u],
+                ALU.add,
+            )
+
+        def z_quantise(u):
+            nc.vector.quantize_mx(out=z_codes[u][:].bitcast(FP8X4), scales=z_scales[u][:], in_=z_bf[u][:])
+
+        def z2_product(h):
+            nc.vector.tensor_tensor(
+                z2_bf[h][:].rearrange("p (c i t) -> p c t i", i=4, t=PACK),
+                inv[:, h * PACK * HALF : (h + 1) * PACK * HALF].rearrange("p (t c i) -> p c t i", t=PACK, i=4),
+                y_gb[:].rearrange("p (t h c i) -> p h c t i", t=PACK, h=2, i=4)[:, h],
+                ALU.mult,
+            )
+
+        def z2_quantise(h):
+            nc.vector.quantize_mx(out=z2_codes[:, cols(h)].bitcast(FP8X4), scales=z2_scales[:, cols(h)], in_=z2_bf[h][:])
+
+        def s_product(t, n_cols):
+            m_cols = slice((t % 2) * P, (t % 2 + 1) * P)
+            nc.tensor.matmul_mx(
+                out=s_ps[t][:, n_cols], lhsT=z_codes[t // 2][:, m_cols].bitcast(FP8X4), lhsT_scale=z_scales[t // 2][:, m_cols],
+                rhs=z2_codes[:, n_cols].bitcast(FP8X4), rhs_scale=z2_scales[:, n_cols], start=True, stop=True,
+            )
+
+        def s_copy(t, n_cols):
+            nc.scalar.activation(s[t][:, n_cols], s_ps[t][:, n_cols], ACT.Copy, scale=0.0625)
+
+        z_sum(0)
+        z2_product(0)
+        z_quantise(0)
+        z2_quantise(0)
+        for t in range(2):
+            s_product(t, cols(0))
+            s_copy(t, cols(0))
+        z2_product(1)
+        z2_quantise(1)
+        for t in range(2):
+            s_product(t, cols(1))
+        z_sum(1)
+        z_quantise(1)
+        for t in range(2, PACK):
+            s_product(t, slice(0, S))
+
+        gate = sb.tile([P, PACK * S], F32, name="gate")
+        st = [sb.tile([P, S], F32, name=f"st{t}") for t in range(PACK)]
+        st_n5 = sb.tile([P, PACK * S], F32, name="st_n5")
+        res = sb.tile([P, PACK * S], F32, name="res")
+        out_rows = out.rearrange("(p t) j -> p t j", t=PACK)
+
+        def gate_and_st(t):
+            s_copy(t, cols(1) if t < 2 else slice(0, S))
+            for h in range(2):
+                nc.scalar.activation(gate[:, plane(t, h)], look_up(s[t], n5_t, h), ACT.Sigmoid)
+                nc.vector.tensor_tensor(st[t][:, cols(h)], s[t][:, cols(h)], gate[:, plane(t, h)], ALU.mult)
+
+        def fetch(t):
+            for h in range(2):
+                nc.vector.tensor_copy(st_n5[:, plane(t, h)], look_up(st[t], n5_t, h))
+
+        def finish(t):
+            for h in range(2):
+                nc.vector.tensor_tensor(res[:, plane(t, h)], st[t][:, cols(h)], st_n5[:, plane(t, h)], ALU.max)
+                nc.sync.dma_start(out_rows[:, t, cols(h)], res[:, plane(t, h)])
+
+        gate_and_st(0)
+        fetch(0)
+        for t in range(1, PACK):
+            gate_and_st(t)
+            finish(t - 1)
+            fetch(t)
+        finish(PACK - 1)

@@ -45,7 +45,9 @@ def tile_picked_selfwsumnormtwicp_none_p_kernel(
                 return slice(t * S, (t + 1) * S)
             return slice(t * S + h * HALF, t * S + (h + 1) * HALF)
 
-        def look_up(window, idx, h):
+        def look_up(window, idx, h=None):
+            if h is None:
+                return window[:].indirect(idx[:])
             return window[:].indirect(idx[:, h * LIST_HALF : (h + 1) * LIST_HALF])
 
         xs_all = sb.tile([P, T], U8, name="xs_all")
@@ -55,14 +57,10 @@ def tile_picked_selfwsumnormtwicp_none_p_kernel(
             nc.scalar.dma_start(
                 xs_all[32 * q : 32 * q + 4, :].bitcast(I32), x_scales[0, 4 * q : 4 * q + 4, :].bitcast(I32)
             )
+        w_raw = sb.tile([P, PACK * S], F32, name="w_raw")
+        nc.sync.dma_start(w_raw[:], w1.rearrange("(p j) c -> p (j c)", j=PACK))
         xw_all = sb.tile([P, T], I32, name="xw_all")
         nc.sync.dma_start(xw_all[:], x_words[0].rearrange("p c r -> p (c r)").bitcast(I32))
-        w_rows = w1.rearrange("(p j) c -> p j c", j=PACK)
-        w_raw = []
-        for h in range(2):
-            tile = sb.tile([P, PACK, HALF], F32, name=f"w_raw{h}")
-            nc.sync.dma_start(tile[:], w_rows[:, :, cols(h)])
-            w_raw.append(tile)
         ga_t = sb.tile([P, PACK], F32, name="ga_t")
         nc.sync.dma_start(ga_t[:], ga.rearrange("(p t) o -> p (t o)", t=PACK))
         gb_t = sb.tile([P, PACK], F32, name="gb_t")
@@ -73,46 +71,51 @@ def tile_picked_selfwsumnormtwicp_none_p_kernel(
         n4_t = load_list("n4_t", n4)
         n5_t = load_list("n5_t", n5)
 
+        warm_in = sb.tile([P, 1], F32, name="warm_in")
+        nc.gpsimd.memset(warm_in[:], 1.0)
+        warm_out = sb.tile([P, 1], F32, name="warm_out")
+        nc.scalar.activation(warm_out[:], warm_in[:], ACT.Ln)
+
         xs = sb.tile([P, S], U8, name="xs", align_bytes=64)
         nc.vector.tensor_copy(xs[:], xs_all[:].indirect(offs_t[:]))
-        xw = sb.tile([P, S], U32, name="xw", align_bytes=64)
-        nc.vector.tensor_copy(xw[:], xw_all[:].bitcast(U32).indirect(offs_t[:]))
 
         w_bf = sb.tile([P, PACK * S], BF16, name="w_bf", align_bytes=64)
         w_dst = w_bf[:].rearrange("p (t h m j) -> p h m j t", t=PACK, h=2, j=PACK)
-        nc.scalar.copy(w_dst[:, 0], w_raw[0][:].rearrange("p j (m t) -> p m j t", t=PACK))
-        nc.vector.tensor_copy(w_dst[:, 1], w_raw[1][:].rearrange("p j (m t) -> p m j t", t=PACK))
+        w_src = w_raw[:].rearrange("p (j h m t) -> p h m j t", j=PACK, h=2, t=PACK)
+        nc.scalar.copy(w_dst[:, 0], w_src[:, 0])
+        nc.vector.tensor_copy(w_dst[:, 1], w_src[:, 1])
         w_codes = sb.tile([P, S], U32, name="w_codes", align_bytes=64)
         w_scales = sb.tile([P, S], U8, name="w_scales", align_bytes=64)
-        y_ps = []
-        for t in range(PACK):
-            m_cols = slice(t * P, (t + 1) * P)
-            nc.vector.quantize_mx(out=w_codes[:, m_cols].bitcast(FP8X4), scales=w_scales[:, m_cols], in_=w_bf[:, plane(t)])
-            bank = psum.tile([P, S], F32, name=f"y_ps{t}")
-            nc.tensor.matmul_mx(
-                out=bank[:], lhsT=w_codes[:, m_cols].bitcast(FP8X4), lhsT_scale=w_scales[:, m_cols],
-                rhs=xw[:].bitcast(FP8X4), rhs_scale=xs[:], start=True, stop=True,
-            )
-            y_ps.append(bank)
+        nc.vector.quantize_mx(out=w_codes[:].bitcast(FP8X4), scales=w_scales[:], in_=w_bf[:])
+        xw = sb.tile([P, S], U32, name="xw", align_bytes=64)
+        y_ps = [psum.tile([P, S], F32, name=f"y_ps{t}") for t in range(PACK)]
+        for h in range(2):
+            nc.vector.tensor_copy(xw[:, cols(h)], xw_all[:].bitcast(U32).indirect(offs_t[:, h * LIST_HALF : (h + 1) * LIST_HALF]))
+            for t in range(PACK):
+                m_cols = slice(t * P, (t + 1) * P)
+                nc.tensor.matmul_mx(
+                    out=y_ps[t][:, cols(h)], lhsT=w_codes[:, m_cols].bitcast(FP8X4), lhsT_scale=w_scales[:, m_cols],
+                    rhs=xw[:, cols(h)].bitcast(FP8X4), rhs_scale=xs[:, cols(h)], start=True, stop=True,
+                )
 
-        y = [sb.tile([P, S], F32, name=f"y{t}") for t in range(PACK)]
+        y = [sb.tile([P, 2 * S], F32, name=f"y{t}") for t in range(PACK)]
         ln2y = [sb.tile([P, S], F32, name=f"ln2y{t}") for t in range(PACK)]
         y_abs = sb.tile([P, PACK * S], F32, name="y_abs", tag="act")
         for t in range(PACK):
             if t % 2 == 0:
                 nc.scalar.activation(y_abs[:, plane(t)], y_ps[t][:], ACT.Abs)
             else:
-                nc.vector.tensor_copy(y[t][:], y_ps[t][:])
-                nc.vector.scalar_tensor_tensor(y_abs[:, plane(t)], y_ps[t][:], -1.0, y[t][:], ALU.mult, ALU.max)
+                nc.vector.tensor_copy(y[t][:, :S], y_ps[t][:])
+                nc.vector.scalar_tensor_tensor(y_abs[:, plane(t)], y_ps[t][:], -1.0, y[t][:, :S], ALU.mult, ALU.max)
             nc.scalar.activation(ln2y[t][:], y_abs[:, plane(t)], ACT.Ln, bias=TINY, scale=2.0)
         for t in range(0, PACK, 2):
-            nc.vector.tensor_copy(y[t][:], y_ps[t][:])
-        y_ga = [sb.tile([P, S], F32, name=f"y_ga{t}") for t in range(PACK)]
+            nc.vector.tensor_copy(y[t][:, :S], y_ps[t][:])
+        y_ga = [sb.tile([P, 2 * S], F32, name=f"y_ga{t}") for t in range(PACK)]
         y_gb = sb.tile([P, PACK * S], F32, name="y_gb")
         for t in range(PACK):
-            nc.vector.tensor_scalar(y_ga[t][:], y[t][:], ga_t[:, t : t + 1], None, ALU.mult)
+            nc.vector.tensor_scalar(y_ga[t][:, :S], y[t][:, :S], ga_t[:, t : t + 1], None, ALU.mult)
         for t in range(PACK):
-            nc.vector.tensor_scalar(y_gb[:, plane(t)], y[t][:], gb_t[:, t : t + 1], 2.0, ALU.mult, ALU.mult)
+            nc.vector.tensor_scalar(y_gb[:, plane(t)], y[t][:, :S], gb_t[:, t : t + 1], 2.0, ALU.mult, ALU.mult)
 
         sig = sb.tile([P, 3 * PACK * S], F32, name="sig", tag="act")
         sig_y = sig[:, 0 : PACK * S]
@@ -121,13 +124,10 @@ def tile_picked_selfwsumnormtwicp_none_p_kernel(
         prod1 = sb.tile([P, PACK * S], F32, name="prod1")
         prod2 = sb.tile([P, PACK * S], F32, name="prod2")
         for t in range(PACK):
-            nc.scalar.activation(sig_y[:, plane(t)], y[t][:], ACT.Sigmoid)
-            for h in range(2):
-                nc.scalar.activation(sig_n3[:, plane(t, h)], look_up(y[t], n3_t, h), ACT.Sigmoid)
-            for h in range(2):
-                nc.vector.tensor_tensor(prod1[:, plane(t, h)], look_up(y_ga[t], n1_t, h), sig_y[:, plane(t, h)], ALU.mult)
-            for h in range(2):
-                nc.vector.tensor_tensor(prod2[:, plane(t, h)], look_up(y_ga[t], n2_t, h), sig_n3[:, plane(t, h)], ALU.mult)
+            nc.scalar.activation(sig_y[:, plane(t)], y[t][:, :S], ACT.Sigmoid)
+            nc.scalar.activation(sig_n3[:, plane(t)], look_up(y[t], n3_t), ACT.Sigmoid)
+            nc.vector.tensor_tensor(prod1[:, plane(t)], look_up(y_ga[t], n1_t), sig_y[:, plane(t)], ALU.mult)
+            nc.vector.tensor_tensor(prod2[:, plane(t)], look_up(y_ga[t], n2_t), sig_n3[:, plane(t)], ALU.mult)
         for h in range(2):
             for t in range(PACK):
                 lo = (h * PACK + t) * HALF
@@ -140,7 +140,7 @@ def tile_picked_selfwsumnormtwicp_none_p_kernel(
         z_bf = [sb.tile([P, 2 * S], BF16, name=f"z_bf{u}", align_bytes=64) for u in range(2)]
         z2_bf = [sb.tile([P, 2 * S], BF16, name=f"z2_bf{h}", align_bytes=64) for h in range(2)]
         s_ps = [psum.tile([P, S], F32, name=f"s_ps{t}") for t in range(PACK)]
-        s = [sb.tile([P, S], F32, name=f"s{t}") for t in range(PACK)]
+        s = [sb.tile([P, 2 * S], F32, name=f"s{t}") for t in range(PACK)]
 
         def z_sum(u):
             pattern = "p (t m u v) -> p u m t v"
@@ -192,25 +192,27 @@ def tile_picked_selfwsumnormtwicp_none_p_kernel(
             s_product(t, slice(0, S))
 
         gate = sb.tile([P, PACK * S], F32, name="gate")
-        st = [sb.tile([P, S], F32, name=f"st{t}") for t in range(PACK)]
+        st = [sb.tile([P, 2 * S], F32, name=f"st{t}") for t in range(PACK)]
         st_n5 = sb.tile([P, PACK * S], F32, name="st_n5")
         res = sb.tile([P, PACK * S], F32, name="res")
         out_rows = out.rearrange("(p t) j -> p t j", t=PACK)
 
         def gate_and_st(t):
             s_copy(t, cols(1) if t < 2 else slice(0, S))
-            for h in range(2):
+            for h in range(2) if t == 0 else (None,):
+                n_cols = slice(0, S) if h is None else cols(h)
                 nc.scalar.activation(gate[:, plane(t, h)], look_up(s[t], n5_t, h), ACT.Sigmoid)
-                nc.vector.tensor_tensor(st[t][:, cols(h)], s[t][:, cols(h)], gate[:, plane(t, h)], ALU.mult)
+                nc.vector.tensor_tensor(st[t][:, n_cols], s[t][:, n_cols], gate[:, plane(t, h)], ALU.mult)
 
         def fetch(t):
-            for h in range(2):
+            for h in range(2) if t == PACK - 1 else (None,):
                 nc.vector.tensor_copy(st_n5[:, plane(t, h)], look_up(st[t], n5_t, h))
 
         def finish(t):
-            for h in range(2):
-                nc.vector.tensor_tensor(res[:, plane(t, h)], st[t][:, cols(h)], st_n5[:, plane(t, h)], ALU.max)
-                nc.sync.dma_start(out_rows[:, t, cols(h)], res[:, plane(t, h)])
+            for h in range(2) if t == PACK - 1 else (None,):
+                n_cols = slice(0, S) if h is None else cols(h)
+                nc.vector.tensor_tensor(res[:, plane(t, h)], st[t][:, n_cols], st_n5[:, plane(t, h)], ALU.max)
+                nc.sync.dma_start(out_rows[:, t, n_cols], res[:, plane(t, h)])
 
         gate_and_st(0)
         fetch(0)

@@ -50,21 +50,21 @@ def tile_picked_selfwsumnormtwicp_none_p_kernel(
                 return window[:].indirect(idx[:])
             return window[:].indirect(idx[:, h * LIST_HALF : (h + 1) * LIST_HALF])
 
-        xs_all = sb.tile([P, T], U8, name="xs_all")
-        nc.vector.memset(xs_all[:].bitcast(I32), 0)
+        xs_all = sb.tile([P, T], U8, name="xs_all", tag="scale_rows", align_bytes=64)
+        nc.gpsimd.memset(xs_all[:].bitcast(I32), 0)
         offs_t = load_list("offs_t", offs)
-        for q in range(4):
-            nc.scalar.dma_start(
-                xs_all[32 * q : 32 * q + 4, :].bitcast(I32), x_scales[0, 4 * q : 4 * q + 4, :].bitcast(I32)
-            )
         w_raw = sb.tile([P, PACK * S], F32, name="w_raw")
         nc.sync.dma_start(w_raw[:], w1.rearrange("(p j) c -> p (j c)", j=PACK))
-        xw_all = sb.tile([P, T], I32, name="xw_all")
-        nc.sync.dma_start(xw_all[:], x_words[0].rearrange("p c r -> p (c r)").bitcast(I32))
         ga_t = sb.tile([P, PACK], F32, name="ga_t")
         nc.sync.dma_start(ga_t[:], ga.rearrange("(p t) o -> p (t o)", t=PACK))
         gb_t = sb.tile([P, PACK], F32, name="gb_t")
         nc.sync.dma_start(gb_t[:], gb.rearrange("(p t) o -> p (t o)", t=PACK))
+        for q in range(4):
+            nc.sync.dma_start(
+                xs_all[32 * q : 32 * q + 4, :].bitcast(I32), x_scales[0, 4 * q : 4 * q + 4, :].bitcast(I32)
+            )
+        xw_all = sb.tile([P, T], I32, name="xw_all")
+        nc.sync.dma_start(xw_all[:], x_words[0].rearrange("p c r -> p (c r)").bitcast(I32))
         n1_t = load_list("n1_t", n1)
         n3_t = load_list("n3_t", n3)
         n2_t = load_list("n2_t", n2)
@@ -72,7 +72,7 @@ def tile_picked_selfwsumnormtwicp_none_p_kernel(
         n5_t = load_list("n5_t", n5)
 
         warm_in = sb.tile([P, 1], F32, name="warm_in")
-        nc.gpsimd.memset(warm_in[:], 1.0)
+        nc.vector.memset(warm_in[:], 1.0)
         warm_out = sb.tile([P, 1], F32, name="warm_out")
         nc.scalar.activation(warm_out[:], warm_in[:], ACT.Ln)
 
@@ -85,31 +85,47 @@ def tile_picked_selfwsumnormtwicp_none_p_kernel(
         nc.scalar.copy(w_dst[:, 0], w_src[:, 0])
         nc.vector.tensor_copy(w_dst[:, 1], w_src[:, 1])
         w_codes = sb.tile([P, S], U32, name="w_codes", align_bytes=64)
-        w_scales = sb.tile([P, S], U8, name="w_scales", align_bytes=64)
+        w_scales = sb.tile([P, S], U8, name="w_scales", tag="scale_rows", align_bytes=64)
         nc.vector.quantize_mx(out=w_codes[:].bitcast(FP8X4), scales=w_scales[:], in_=w_bf[:])
         xw = sb.tile([P, S], U32, name="xw", align_bytes=64)
-        y_ps = [psum.tile([P, S], F32, name=f"y_ps{t}") for t in range(PACK)]
         for h in range(2):
-            nc.vector.tensor_copy(xw[:, cols(h)], xw_all[:].bitcast(U32).indirect(offs_t[:, h * LIST_HALF : (h + 1) * LIST_HALF]))
-            for t in range(PACK):
-                m_cols = slice(t * P, (t + 1) * P)
-                nc.tensor.matmul_mx(
-                    out=y_ps[t][:, cols(h)], lhsT=w_codes[:, m_cols].bitcast(FP8X4), lhsT_scale=w_scales[:, m_cols],
-                    rhs=xw[:, cols(h)].bitcast(FP8X4), rhs_scale=xs[:, cols(h)], start=True, stop=True,
-                )
+            nc.vector.tensor_copy(xw[:, cols(h)], look_up(xw_all[:].bitcast(U32), offs_t, h))
+
+        def y_product(bank, t, n_cols):
+            m_cols = slice(t * P, (t + 1) * P)
+            nc.tensor.matmul_mx(
+                out=bank[:], lhsT=w_codes[:, m_cols].bitcast(FP8X4), lhsT_scale=w_scales[:, m_cols],
+                rhs=xw[:, n_cols].bitcast(FP8X4), rhs_scale=xs[:, n_cols], start=True, stop=True,
+            )
+
+        y_half_ps = {}
+        for h in range(2):
+            for t in range(2):
+                y_half_ps[t, h] = psum.tile([P, HALF], F32, name=f"y_ps{t}{h}")
+                y_product(y_half_ps[t, h], t, cols(h))
+        y_ps = {}
+        for t in range(2, PACK):
+            y_ps[t] = psum.tile([P, S], F32, name=f"y_ps{t}", tag=f"bank{t}")
+            y_product(y_ps[t], t, slice(0, S))
 
         y = [sb.tile([P, 2 * S], F32, name=f"y{t}") for t in range(PACK)]
         ln2y = [sb.tile([P, S], F32, name=f"ln2y{t}") for t in range(PACK)]
         y_abs = sb.tile([P, PACK * S], F32, name="y_abs", tag="act")
-        for t in range(PACK):
-            if t % 2 == 0:
-                nc.scalar.activation(y_abs[:, plane(t)], y_ps[t][:], ACT.Abs)
-            else:
-                nc.vector.tensor_copy(y[t][:, :S], y_ps[t][:])
-                nc.vector.scalar_tensor_tensor(y_abs[:, plane(t)], y_ps[t][:], -1.0, y[t][:, :S], ALU.mult, ALU.max)
+
+        def log_of(t):
             nc.scalar.activation(ln2y[t][:], y_abs[:, plane(t)], ACT.Ln, bias=TINY, scale=2.0)
-        for t in range(0, PACK, 2):
-            nc.vector.tensor_copy(y[t][:, :S], y_ps[t][:])
+
+        for h in range(2):
+            for t in range(2):
+                nc.scalar.activation(y_abs[:, plane(t, h)], y_half_ps[t, h][:], ACT.Abs)
+                nc.vector.tensor_copy(y[t][:, cols(h)], y_half_ps[t, h][:])
+        nc.vector.tensor_copy(y[2][:, :S], y_ps[2][:])
+        nc.vector.scalar_tensor_tensor(y_abs[:, plane(2)], y_ps[2][:], -1.0, y[2][:, :S], ALU.mult, ALU.max)
+        log_of(0)
+        nc.scalar.activation(y_abs[:, plane(3)], y_ps[3][:], ACT.Abs)
+        for t in (1, 3, 2):
+            log_of(t)
+        nc.vector.tensor_copy(y[3][:, :S], y_ps[3][:])
         y_ga = [sb.tile([P, 2 * S], F32, name=f"y_ga{t}") for t in range(PACK)]
         y_gb = sb.tile([P, PACK * S], F32, name="y_gb")
         for t in range(PACK):
@@ -124,9 +140,11 @@ def tile_picked_selfwsumnormtwicp_none_p_kernel(
         prod1 = sb.tile([P, PACK * S], F32, name="prod1")
         prod2 = sb.tile([P, PACK * S], F32, name="prod2")
         for t in range(PACK):
-            nc.scalar.activation(sig_y[:, plane(t)], y[t][:, :S], ACT.Sigmoid)
+            for h in range(2) if t == 0 else (None,):
+                n_cols = slice(0, S) if h is None else cols(h)
+                nc.scalar.activation(sig_y[:, plane(t, h)], y[t][:, n_cols], ACT.Sigmoid)
+                nc.vector.tensor_tensor(prod1[:, plane(t, h)], look_up(y_ga[t], n1_t, h), sig_y[:, plane(t, h)], ALU.mult)
             nc.scalar.activation(sig_n3[:, plane(t)], look_up(y[t], n3_t), ACT.Sigmoid)
-            nc.vector.tensor_tensor(prod1[:, plane(t)], look_up(y_ga[t], n1_t), sig_y[:, plane(t)], ALU.mult)
             nc.vector.tensor_tensor(prod2[:, plane(t)], look_up(y_ga[t], n2_t), sig_n3[:, plane(t)], ALU.mult)
         for h in range(2):
             for t in range(PACK):
@@ -139,7 +157,7 @@ def tile_picked_selfwsumnormtwicp_none_p_kernel(
         z2_scales = sb.tile([P, S], U8, name="z2_scales", align_bytes=64)
         z_bf = [sb.tile([P, 2 * S], BF16, name=f"z_bf{u}", align_bytes=64) for u in range(2)]
         z2_bf = [sb.tile([P, 2 * S], BF16, name=f"z2_bf{h}", align_bytes=64) for h in range(2)]
-        s_ps = [psum.tile([P, S], F32, name=f"s_ps{t}") for t in range(PACK)]
+        s_ps = [psum.tile([P, S], F32, name=f"s_ps{t}", tag=f"bank{t}") for t in range(PACK)]
         s = [sb.tile([P, 2 * S], F32, name=f"s{t}") for t in range(PACK)]
 
         def z_sum(u):

@@ -16,9 +16,14 @@ P = 128
 PACK = 4
 T = 2048
 S = 512
-HALF = S // 2
-LIST_HALF = HALF // 16
+LIST_ROWS = 16
+LINE = 4
 TINY = 2.0 ** -60
+S_SCALE = 0.0625
+
+WHOLE = slice(0, S)
+HALVES = (slice(0, S // 2), slice(S // 2, S))
+LAST = PACK - 1
 
 FLOPS = 2 * 2 * 512 * 512 * 512
 
@@ -33,38 +38,31 @@ def tile_picked_selfwsumnormtwicp_none_p_kernel(
         psum = ctx.enter_context(tc.psum_pool(name="psum", bufs=1))
 
         def load_list(name, src):
-            tile = lists.tile([P, S // 16], U16, name=name)
+            tile = lists.tile([P, S // LIST_ROWS], U16, name=name)
             nc.sync.dma_start(tile[:], src)
             return tile
 
-        def cols(h):
-            return slice(h * HALF, (h + 1) * HALF)
+        def look_up(window, list_tile, cols):
+            return window[:].indirect(list_tile[:, cols.start // LIST_ROWS : cols.stop // LIST_ROWS])
 
-        def plane(t, h=None):
-            if h is None:
-                return slice(t * S, (t + 1) * S)
-            return slice(t * S + h * HALF, t * S + (h + 1) * HALF)
-
-        def look_up(window, idx, h=None):
-            if h is None:
-                return window[:].indirect(idx[:])
-            return window[:].indirect(idx[:, h * LIST_HALF : (h + 1) * LIST_HALF])
+        def in_tile(t, cols):
+            return slice(t * S + cols.start, t * S + cols.stop)
 
         xs_all = sb.tile([P, T], U8, name="xs_all", tag="scale_rows", align_bytes=64)
         nc.gpsimd.memset(xs_all[:].bitcast(I32), 0)
         offs_t = load_list("offs_t", offs)
         w_raw = sb.tile([P, PACK * S], F32, name="w_raw")
         nc.sync.dma_start(w_raw[:], w1.rearrange("(p j) c -> p (j c)", j=PACK))
-        ga_t = sb.tile([P, PACK], F32, name="ga_t")
-        nc.sync.dma_start(ga_t[:], ga.rearrange("(p t) o -> p (t o)", t=PACK))
-        gb_t = sb.tile([P, PACK], F32, name="gb_t")
-        nc.sync.dma_start(gb_t[:], gb.rearrange("(p t) o -> p (t o)", t=PACK))
         for q in range(4):
             nc.sync.dma_start(
                 xs_all[32 * q : 32 * q + 4, :].bitcast(I32), x_scales[0, 4 * q : 4 * q + 4, :].bitcast(I32)
             )
         xw_all = sb.tile([P, T], I32, name="xw_all")
         nc.sync.dma_start(xw_all[:], x_words[0].rearrange("p c r -> p (c r)").bitcast(I32))
+        ga_t = sb.tile([P, PACK], F32, name="ga_t")
+        nc.sync.dma_start(ga_t[:], ga.rearrange("(p t) o -> p (t o)", t=PACK))
+        gb_t = sb.tile([P, PACK], F32, name="gb_t")
+        nc.sync.dma_start(gb_t[:], gb.rearrange("(p t) o -> p (t o)", t=PACK))
         n1_t = load_list("n1_t", n1)
         n3_t = load_list("n3_t", n3)
         n2_t = load_list("n2_t", n2)
@@ -77,7 +75,7 @@ def tile_picked_selfwsumnormtwicp_none_p_kernel(
         nc.scalar.activation(warm_out[:], warm_in[:], ACT.Ln)
 
         xs = sb.tile([P, S], U8, name="xs", align_bytes=64)
-        nc.vector.tensor_copy(xs[:], xs_all[:].indirect(offs_t[:]))
+        nc.vector.tensor_copy(xs[:], look_up(xs_all, offs_t, WHOLE))
 
         w_bf = sb.tile([P, PACK * S], BF16, name="w_bf", align_bytes=64)
         w_dst = w_bf[:].rearrange("p (t h m j) -> p h m j t", t=PACK, h=2, j=PACK)
@@ -87,81 +85,95 @@ def tile_picked_selfwsumnormtwicp_none_p_kernel(
         w_codes = sb.tile([P, S], U32, name="w_codes", align_bytes=64)
         w_scales = sb.tile([P, S], U8, name="w_scales", tag="scale_rows", align_bytes=64)
         nc.vector.quantize_mx(out=w_codes[:].bitcast(FP8X4), scales=w_scales[:], in_=w_bf[:])
-        xw = sb.tile([P, S], U32, name="xw", align_bytes=64)
-        for h in range(2):
-            nc.vector.tensor_copy(xw[:, cols(h)], look_up(xw_all[:].bitcast(U32), offs_t, h))
 
-        def y_product(bank, t, n_cols):
+        xw = sb.tile([P, S], U32, name="xw", align_bytes=64)
+        for cols in HALVES:
+            nc.vector.tensor_copy(xw[:, cols], look_up(xw_all[:].bitcast(U32), offs_t, cols))
+
+        def y_product(bank, t, cols):
             m_cols = slice(t * P, (t + 1) * P)
             nc.tensor.matmul_mx(
-                out=bank[:], lhsT=w_codes[:, m_cols].bitcast(FP8X4), lhsT_scale=w_scales[:, m_cols],
-                rhs=xw[:, n_cols].bitcast(FP8X4), rhs_scale=xs[:, n_cols], start=True, stop=True,
+                out=bank[:],
+                lhsT=w_codes[:, m_cols].bitcast(FP8X4),
+                lhsT_scale=w_scales[:, m_cols],
+                rhs=xw[:, cols].bitcast(FP8X4),
+                rhs_scale=xs[:, cols],
+                start=True,
+                stop=True,
             )
 
         y_half_ps = {}
-        for h in range(2):
-            for t in range(2):
-                y_half_ps[t, h] = psum.tile([P, HALF], F32, name=f"y_ps{t}{h}")
-                y_product(y_half_ps[t, h], t, cols(h))
+        for h, cols in enumerate(HALVES):
+            for t in (0, 1):
+                y_half_ps[t, h] = psum.tile([P, S // 2], F32, name=f"y_ps{t}{h}")
+                y_product(y_half_ps[t, h], t, cols)
         y_ps = {}
-        for t in range(2, PACK):
+        for t in (2, 3):
             y_ps[t] = psum.tile([P, S], F32, name=f"y_ps{t}", tag=f"bank{t}")
-            y_product(y_ps[t], t, slice(0, S))
+            y_product(y_ps[t], t, WHOLE)
 
         y = [sb.tile([P, 2 * S], F32, name=f"y{t}") for t in range(PACK)]
         ln2y = [sb.tile([P, S], F32, name=f"ln2y{t}") for t in range(PACK)]
-        y_abs = sb.tile([P, PACK * S], F32, name="y_abs", tag="act")
+        y_abs = sb.tile([P, PACK * S], F32, name="y_abs", tag="scalar_out")
 
         def log_of(t):
-            nc.scalar.activation(ln2y[t][:], y_abs[:, plane(t)], ACT.Ln, bias=TINY, scale=2.0)
+            nc.scalar.activation(ln2y[t][:], y_abs[:, in_tile(t, WHOLE)], ACT.Ln, bias=TINY, scale=2.0)
 
-        for h in range(2):
-            for t in range(2):
-                nc.scalar.activation(y_abs[:, plane(t, h)], y_half_ps[t, h][:], ACT.Abs)
-                nc.vector.tensor_copy(y[t][:, cols(h)], y_half_ps[t, h][:])
-        nc.vector.tensor_copy(y[2][:, :S], y_ps[2][:])
-        nc.vector.scalar_tensor_tensor(y_abs[:, plane(2)], y_ps[2][:], -1.0, y[2][:, :S], ALU.mult, ALU.max)
+        for h, cols in enumerate(HALVES):
+            for t in (0, 1):
+                nc.scalar.activation(y_abs[:, in_tile(t, cols)], y_half_ps[t, h][:], ACT.Abs)
+                nc.vector.tensor_copy(y[t][:, cols], y_half_ps[t, h][:])
+        nc.vector.tensor_copy(y[2][:, WHOLE], y_ps[2][:])
+        nc.vector.scalar_tensor_tensor(y_abs[:, in_tile(2, WHOLE)], y_ps[2][:], -1.0, y[2][:, WHOLE], ALU.mult, ALU.max)
         log_of(0)
-        nc.scalar.activation(y_abs[:, plane(3)], y_ps[3][:], ACT.Abs)
+        nc.scalar.activation(y_abs[:, in_tile(3, WHOLE)], y_ps[3][:], ACT.Abs)
         for t in (1, 3, 2):
             log_of(t)
-        nc.vector.tensor_copy(y[3][:, :S], y_ps[3][:])
+        nc.vector.tensor_copy(y[3][:, WHOLE], y_ps[3][:])
+
         y_ga = [sb.tile([P, 2 * S], F32, name=f"y_ga{t}") for t in range(PACK)]
         y_gb = sb.tile([P, PACK * S], F32, name="y_gb")
         for t in range(PACK):
-            nc.vector.tensor_scalar(y_ga[t][:, :S], y[t][:, :S], ga_t[:, t : t + 1], None, ALU.mult)
+            nc.vector.tensor_scalar(y_ga[t][:, WHOLE], y[t][:, WHOLE], ga_t[:, t : t + 1], None, ALU.mult)
         for t in range(PACK):
-            nc.vector.tensor_scalar(y_gb[:, plane(t)], y[t][:, :S], gb_t[:, t : t + 1], 2.0, ALU.mult, ALU.mult)
+            nc.vector.tensor_scalar(y_gb[:, in_tile(t, WHOLE)], y[t][:, WHOLE], gb_t[:, t : t + 1], 2.0, ALU.mult, ALU.mult)
 
-        sig = sb.tile([P, 3 * PACK * S], F32, name="sig", tag="act")
+        sig = sb.tile([P, 3 * PACK * S], F32, name="sig", tag="scalar_out")
         sig_y = sig[:, 0 : PACK * S]
         sig_n3 = sig[:, PACK * S : 2 * PACK * S]
-        inv = sig[:, 2 * PACK * S : 3 * PACK * S]
+        half_inv = sig[:, 2 * PACK * S : 3 * PACK * S]
         prod1 = sb.tile([P, PACK * S], F32, name="prod1")
         prod2 = sb.tile([P, PACK * S], F32, name="prod2")
         for t in range(PACK):
-            for h in range(2) if t == 0 else (None,):
-                n_cols = slice(0, S) if h is None else cols(h)
-                nc.scalar.activation(sig_y[:, plane(t, h)], y[t][:, n_cols], ACT.Sigmoid)
-                nc.vector.tensor_tensor(prod1[:, plane(t, h)], look_up(y_ga[t], n1_t, h), sig_y[:, plane(t, h)], ALU.mult)
-            nc.scalar.activation(sig_n3[:, plane(t)], look_up(y[t], n3_t), ACT.Sigmoid)
-            nc.vector.tensor_tensor(prod2[:, plane(t)], look_up(y_ga[t], n2_t), sig_n3[:, plane(t)], ALU.mult)
-        for h in range(2):
+            for cols in HALVES if t == 0 else (WHOLE,):
+                nc.scalar.activation(sig_y[:, in_tile(t, cols)], y[t][:, cols], ACT.Sigmoid)
+                nc.vector.tensor_tensor(
+                    prod1[:, in_tile(t, cols)], look_up(y_ga[t], n1_t, cols), sig_y[:, in_tile(t, cols)], ALU.mult
+                )
+            whole = in_tile(t, WHOLE)
+            nc.scalar.activation(sig_n3[:, whole], look_up(y[t], n3_t, WHOLE), ACT.Sigmoid)
+            nc.vector.tensor_tensor(prod2[:, whole], look_up(y_ga[t], n2_t, WHOLE), sig_n3[:, whole], ALU.mult)
+        for cols in HALVES:
+            width = cols.stop - cols.start
             for t in range(PACK):
-                lo = (h * PACK + t) * HALF
-                nc.scalar.activation(inv[:, lo : lo + HALF], look_up(ln2y[t], n4_t, h), ACT.Sigmoid, scale=-1.0)
+                first = PACK * cols.start + t * width
+                nc.scalar.activation(half_inv[:, first : first + width], look_up(ln2y[t], n4_t, cols), ACT.Sigmoid, scale=-1.0)
 
         z_codes = [sb.tile([P, 2 * P], U32, name=f"z_codes{u}", align_bytes=64) for u in range(2)]
         z_scales = [sb.tile([P, 2 * P], U8, name=f"z_scales{u}", align_bytes=64) for u in range(2)]
         z2_codes = sb.tile([P, S], U32, name="z2_codes", align_bytes=64)
         z2_scales = sb.tile([P, S], U8, name="z2_scales", align_bytes=64)
-        z_bf = [sb.tile([P, 2 * S], BF16, name=f"z_bf{u}", align_bytes=64) for u in range(2)]
-        z2_bf = [sb.tile([P, 2 * S], BF16, name=f"z2_bf{h}", align_bytes=64) for h in range(2)]
         s_ps = [psum.tile([P, S], F32, name=f"s_ps{t}", tag=f"bank{t}") for t in range(PACK)]
         s = [sb.tile([P, 2 * S], F32, name=f"s{t}") for t in range(PACK)]
 
+        z_bf, z2_bf = {}, {}
+
+        def rounded_tile(name, tag):
+            return sb.tile([P, 2 * S], BF16, name=name, tag=tag, align_bytes=64)
+
         def z_sum(u):
             pattern = "p (t m u v) -> p u m t v"
+            z_bf[u] = rounded_tile(f"z_bf{u}", tag=f"z_bf{u}")
             nc.vector.tensor_tensor(
                 z_bf[u][:].rearrange("p (v m t) -> p m t v", v=2, t=PACK),
                 prod1[:].rearrange(pattern, t=PACK, u=2, v=2)[:, u],
@@ -172,65 +184,74 @@ def tile_picked_selfwsumnormtwicp_none_p_kernel(
         def z_quantise(u):
             nc.vector.quantize_mx(out=z_codes[u][:].bitcast(FP8X4), scales=z_scales[u][:], in_=z_bf[u][:])
 
-        def z2_product(h):
+        def z2_product(n):
+            cols = HALVES[n]
+            z2_bf[n] = rounded_tile(f"z2_bf{n}", tag="z2_bf0" if n == 0 else "z_bf1")
             nc.vector.tensor_tensor(
-                z2_bf[h][:].rearrange("p (c i t) -> p c t i", i=4, t=PACK),
-                inv[:, h * PACK * HALF : (h + 1) * PACK * HALF].rearrange("p (t c i) -> p c t i", t=PACK, i=4),
-                y_gb[:].rearrange("p (t h c i) -> p h c t i", t=PACK, h=2, i=4)[:, h],
+                z2_bf[n][:].rearrange("p (c i t) -> p c t i", i=LINE, t=PACK),
+                half_inv[:, PACK * cols.start : PACK * cols.stop].rearrange("p (t c i) -> p c t i", t=PACK, i=LINE),
+                y_gb[:].rearrange("p (t c i) -> p c t i", t=PACK, i=LINE)[:, cols.start // LINE : cols.stop // LINE],
                 ALU.mult,
             )
 
-        def z2_quantise(h):
-            nc.vector.quantize_mx(out=z2_codes[:, cols(h)].bitcast(FP8X4), scales=z2_scales[:, cols(h)], in_=z2_bf[h][:])
+        def z2_quantise(n):
+            cols = HALVES[n]
+            nc.vector.quantize_mx(out=z2_codes[:, cols].bitcast(FP8X4), scales=z2_scales[:, cols], in_=z2_bf[n][:])
 
-        def s_product(t, n_cols):
-            m_cols = slice((t % 2) * P, (t % 2 + 1) * P)
+        def s_product(t, cols):
+            u, v = divmod(t, 2)
+            m_cols = slice(v * P, (v + 1) * P)
             nc.tensor.matmul_mx(
-                out=s_ps[t][:, n_cols], lhsT=z_codes[t // 2][:, m_cols].bitcast(FP8X4), lhsT_scale=z_scales[t // 2][:, m_cols],
-                rhs=z2_codes[:, n_cols].bitcast(FP8X4), rhs_scale=z2_scales[:, n_cols], start=True, stop=True,
+                out=s_ps[t][:, cols],
+                lhsT=z_codes[u][:, m_cols].bitcast(FP8X4),
+                lhsT_scale=z_scales[u][:, m_cols],
+                rhs=z2_codes[:, cols].bitcast(FP8X4),
+                rhs_scale=z2_scales[:, cols],
+                start=True,
+                stop=True,
             )
 
-        def s_copy(t, n_cols):
-            nc.scalar.activation(s[t][:, n_cols], s_ps[t][:, n_cols], ACT.Copy, scale=0.0625)
+        def s_copy(t, cols):
+            nc.scalar.activation(s[t][:, cols], s_ps[t][:, cols], ACT.Copy, scale=S_SCALE)
 
         z_sum(0)
         z2_product(0)
         z_quantise(0)
         z2_quantise(0)
-        for t in range(2):
-            s_product(t, cols(0))
-            s_copy(t, cols(0))
+        for t in (0, 1):
+            s_product(t, HALVES[0])
+            s_copy(t, HALVES[0])
         z2_product(1)
         z2_quantise(1)
-        for t in range(2):
-            s_product(t, cols(1))
+        for t in (0, 1):
+            s_product(t, HALVES[1])
         z_sum(1)
         z_quantise(1)
-        for t in range(2, PACK):
-            s_product(t, slice(0, S))
+        for t in (2, 3):
+            s_product(t, WHOLE)
 
-        gate = sb.tile([P, PACK * S], F32, name="gate")
+        gate = sb.tile([P, PACK * S - S // 2], F32, name="gate")
+        gate_first = (S // 2, 0, 3 * S // 2, 5 * S // 2)
         st = [sb.tile([P, 2 * S], F32, name=f"st{t}") for t in range(PACK)]
         st_n5 = sb.tile([P, PACK * S], F32, name="st_n5")
         res = sb.tile([P, PACK * S], F32, name="res")
         out_rows = out.rearrange("(p t) j -> p t j", t=PACK)
 
         def gate_and_st(t):
-            s_copy(t, cols(1) if t < 2 else slice(0, S))
-            for h in range(2) if t == 0 else (None,):
-                n_cols = slice(0, S) if h is None else cols(h)
-                nc.scalar.activation(gate[:, plane(t, h)], look_up(s[t], n5_t, h), ACT.Sigmoid)
-                nc.vector.tensor_tensor(st[t][:, n_cols], s[t][:, n_cols], gate[:, plane(t, h)], ALU.mult)
+            s_copy(t, HALVES[1] if t < 2 else WHOLE)
+            for cols in HALVES if t == 0 else (WHOLE,):
+                gate_t = gate[:, gate_first[t] + cols.start : gate_first[t] + cols.stop]
+                nc.scalar.activation(gate_t, look_up(s[t], n5_t, cols), ACT.Sigmoid)
+                nc.vector.tensor_tensor(st[t][:, cols], s[t][:, cols], gate_t, ALU.mult)
 
         def fetch(t):
-            for h in range(2) if t == PACK - 1 else (None,):
-                nc.vector.tensor_copy(st_n5[:, plane(t, h)], look_up(st[t], n5_t, h))
+            for cols in HALVES if t == LAST else (WHOLE,):
+                nc.vector.tensor_copy(st_n5[:, in_tile(t, cols)], look_up(st[t], n5_t, cols))
 
         def finish(t):
-            for h in range(2) if t == PACK - 1 else (None,):
-                n_cols = slice(0, S) if h is None else cols(h)
-                nc.vector.tensor_tensor(res[:, plane(t, h)], st[t][:, n_cols], st_n5[:, plane(t, h)], ALU.max)
-                nc.sync.dma_start(out_rows[:, t, n_cols], res[:, plane(t, h)])
+            for cols in HALVES if t == LAST else (WHOLE,):
+                nc.vector.tensor_tensor(res[:, in_tile(t, cols)], st[t][:, cols], st_n5[:, in_tile(t, cols)], ALU.max)
+                nc.sync.dma_start(out_rows[:, t, cols], res[:, in_tile(t, cols)])
 
         gate_and_st(0)
         fetch(0)
@@ -238,4 +259,4 @@ def tile_picked_selfwsumnormtwicp_none_p_kernel(
             gate_and_st(t)
             finish(t - 1)
             fetch(t)
-        finish(PACK - 1)
+        finish(LAST)

from contextlib import ExitStack

import concourse.mybir as mybir

F32 = mybir.dt.float32
BF16 = mybir.dt.bfloat16
I32 = mybir.dt.int32
U32 = mybir.dt.uint32
U16 = mybir.dt.uint16
U8 = mybir.dt.uint8
FP8X4 = mybir.dt.float8_e4m3fn_x4
ACT = mybir.ActivationFunctionType
ALU = mybir.AluOpType

P = 128
PACK = 4
T = 2048
S = 512
LIST_ROWS = 16
LINE = 4
TINY = 2.0 ** -60
S_SCALE = 0.0625

WHOLE = slice(0, S)
HALVES = (slice(0, S // 2), slice(S // 2, S))
LAST = PACK - 1

FLOPS = 2 * 2 * 512 * 512 * 512


def tile_picked_selfwsumnormtwicp_none_p_kernel(
    tc, x_words, x_scales, w1, ga, gb, offs, n1, n2, n3, n4, n5, out
):
    nc = tc.nc
    with ExitStack() as ctx:
        lists = ctx.enter_context(tc.tile_pool(name="lists", bufs=1))
        sb = ctx.enter_context(tc.tile_pool(name="sb", bufs=1))
        psum = ctx.enter_context(tc.psum_pool(name="psum", bufs=1))

        def load_list(name, src):
            tile = lists.tile([P, S // LIST_ROWS], U16, name=name)
            nc.sync.dma_start(tile[:], src)
            return tile

        def look_up(window, list_tile, cols):
            return window[:].indirect(list_tile[:, cols.start // LIST_ROWS : cols.stop // LIST_ROWS])

        def in_tile(t, cols):
            return slice(t * S + cols.start, t * S + cols.stop)

        xs_all = sb.tile([P, T], U8, name="xs_all", tag="scale_rows", align_bytes=64)
        nc.gpsimd.memset(xs_all[:].bitcast(I32), 0)
        offs_t = load_list("offs_t", offs)
        w_raw = sb.tile([P, PACK * S], F32, name="w_raw")
        nc.sync.dma_start(w_raw[:], w1.rearrange("(p j) c -> p (j c)", j=PACK))
        for q in range(4):
            nc.sync.dma_start(
                xs_all[32 * q : 32 * q + 4, :].bitcast(I32), x_scales[0, 4 * q : 4 * q + 4, :].bitcast(I32)
            )
        xw_all = sb.tile([P, T], I32, name="xw_all")
        nc.sync.dma_start(xw_all[:], x_words[0].rearrange("p c r -> p (c r)").bitcast(I32))
        ga_t = sb.tile([P, PACK], F32, name="ga_t")
        nc.sync.dma_start(ga_t[:], ga.rearrange("(p t) o -> p (t o)", t=PACK))
        gb_t = sb.tile([P, PACK], F32, name="gb_t")
        nc.sync.dma_start(gb_t[:], gb.rearrange("(p t) o -> p (t o)", t=PACK))
        n1_t = load_list("n1_t", n1)
        n3_t = load_list("n3_t", n3)
        n2_t = load_list("n2_t", n2)
        n4_t = load_list("n4_t", n4)
        n5_t = load_list("n5_t", n5)

        warm_in = sb.tile([P, 1], F32, name="warm_in")
        nc.vector.memset(warm_in[:], 1.0)
        warm_out = sb.tile([P, 1], F32, name="warm_out")
        nc.scalar.activation(warm_out[:], warm_in[:], ACT.Ln)

        xs = sb.tile([P, S], U8, name="xs", align_bytes=64)
        nc.vector.tensor_copy(xs[:], look_up(xs_all, offs_t, WHOLE))

        w_bf = sb.tile([P, PACK * S], BF16, name="w_bf", align_bytes=64)
        w_dst = w_bf[:].rearrange("p (t h m j) -> p h m j t", t=PACK, h=2, j=PACK)
        w_src = w_raw[:].rearrange("p (j h m t) -> p h m j t", j=PACK, h=2, t=PACK)
        nc.scalar.copy(w_dst[:, 0], w_src[:, 0])
        nc.vector.tensor_copy(w_dst[:, 1], w_src[:, 1])
        w_codes = sb.tile([P, S], U32, name="w_codes", align_bytes=64)
        w_scales = sb.tile([P, S], U8, name="w_scales", tag="scale_rows", align_bytes=64)
        nc.vector.quantize_mx(out=w_codes[:].bitcast(FP8X4), scales=w_scales[:], in_=w_bf[:])

        xw = sb.tile([P, S], U32, name="xw", align_bytes=64)
        for cols in HALVES:
            nc.vector.tensor_copy(xw[:, cols], look_up(xw_all[:].bitcast(U32), offs_t, cols))

        def y_product(bank, t, cols):
            m_cols = slice(t * P, (t + 1) * P)
            nc.tensor.matmul_mx(
                out=bank[:],
                lhsT=w_codes[:, m_cols].bitcast(FP8X4),
                lhsT_scale=w_scales[:, m_cols],
                rhs=xw[:, cols].bitcast(FP8X4),
                rhs_scale=xs[:, cols],
                start=True,
                stop=True,
            )

        y_half_ps = {}
        for h, cols in enumerate(HALVES):
            for t in (0, 1):
                y_half_ps[t, h] = psum.tile([P, S // 2], F32, name=f"y_ps{t}{h}")
                y_product(y_half_ps[t, h], t, cols)
        y_ps = {}
        for t in (2, 3):
            y_ps[t] = psum.tile([P, S], F32, name=f"y_ps{t}", tag=f"bank{t}")
            y_product(y_ps[t], t, WHOLE)

        y = [sb.tile([P, 2 * S], F32, name=f"y{t}") for t in range(PACK)]
        ln2y = [sb.tile([P, S], F32, name=f"ln2y{t}") for t in range(PACK)]
        y_abs = sb.tile([P, PACK * S], F32, name="y_abs", tag="scalar_out")

        def log_of(t):
            nc.scalar.activation(ln2y[t][:], y_abs[:, in_tile(t, WHOLE)], ACT.Ln, bias=TINY, scale=2.0)

        for h, cols in enumerate(HALVES):
            for t in (0, 1):
                nc.scalar.activation(y_abs[:, in_tile(t, cols)], y_half_ps[t, h][:], ACT.Abs)
                nc.vector.tensor_copy(y[t][:, cols], y_half_ps[t, h][:])
        nc.vector.tensor_copy(y[2][:, WHOLE], y_ps[2][:])
        nc.vector.scalar_tensor_tensor(y_abs[:, in_tile(2, WHOLE)], y_ps[2][:], -1.0, y[2][:, WHOLE], ALU.mult, ALU.max)
        log_of(0)
        nc.scalar.activation(y_abs[:, in_tile(3, WHOLE)], y_ps[3][:], ACT.Abs)
        for t in (1, 3, 2):
            log_of(t)
        nc.vector.tensor_copy(y[3][:, WHOLE], y_ps[3][:])

        y_ga = [sb.tile([P, 2 * S], F32, name=f"y_ga{t}") for t in range(PACK)]
        y_gb = sb.tile([P, PACK * S], F32, name="y_gb")
        for t in range(PACK):
            nc.vector.tensor_scalar(y_ga[t][:, WHOLE], y[t][:, WHOLE], ga_t[:, t : t + 1], None, ALU.mult)
        for t in range(PACK):
            nc.vector.tensor_scalar(y_gb[:, in_tile(t, WHOLE)], y[t][:, WHOLE], gb_t[:, t : t + 1], 2.0, ALU.mult, ALU.mult)

        sig = sb.tile([P, 3 * PACK * S], F32, name="sig", tag="scalar_out")
        sig_y = sig[:, 0 : PACK * S]
        sig_n3 = sig[:, PACK * S : 2 * PACK * S]
        half_inv = sig[:, 2 * PACK * S : 3 * PACK * S]
        prod1 = sb.tile([P, PACK * S], F32, name="prod1")
        prod2 = sb.tile([P, PACK * S], F32, name="prod2")
        for t in range(PACK):
            for cols in HALVES if t == 0 else (WHOLE,):
                nc.scalar.activation(sig_y[:, in_tile(t, cols)], y[t][:, cols], ACT.Sigmoid)
                nc.vector.tensor_tensor(
                    prod1[:, in_tile(t, cols)], look_up(y_ga[t], n1_t, cols), sig_y[:, in_tile(t, cols)], ALU.mult
                )
            whole = in_tile(t, WHOLE)
            nc.scalar.activation(sig_n3[:, whole], look_up(y[t], n3_t, WHOLE), ACT.Sigmoid)
            nc.vector.tensor_tensor(prod2[:, whole], look_up(y_ga[t], n2_t, WHOLE), sig_n3[:, whole], ALU.mult)
        for cols in HALVES:
            width = cols.stop - cols.start
            for t in range(PACK):
                first = PACK * cols.start + t * width
                nc.scalar.activation(half_inv[:, first : first + width], look_up(ln2y[t], n4_t, cols), ACT.Sigmoid, scale=-1.0)

        z_codes = [sb.tile([P, 2 * P], U32, name=f"z_codes{u}", align_bytes=64) for u in range(2)]
        z_scales = [sb.tile([P, 2 * P], U8, name=f"z_scales{u}", align_bytes=64) for u in range(2)]
        z2_codes = sb.tile([P, S], U32, name="z2_codes", align_bytes=64)
        z2_scales = sb.tile([P, S], U8, name="z2_scales", align_bytes=64)
        s_ps = [psum.tile([P, S], F32, name=f"s_ps{t}", tag=f"bank{t}") for t in range(PACK)]
        s = [sb.tile([P, 2 * S], F32, name=f"s{t}") for t in range(PACK)]

        z_bf, z2_bf = {}, {}

        def rounded_tile(name, tag):
            return sb.tile([P, 2 * S], BF16, name=name, tag=tag, align_bytes=64)

        def z_sum(u):
            pattern = "p (t m u v) -> p u m t v"
            z_bf[u] = rounded_tile(f"z_bf{u}", tag=f"z_bf{u}")
            nc.vector.tensor_tensor(
                z_bf[u][:].rearrange("p (v m t) -> p m t v", v=2, t=PACK),
                prod1[:].rearrange(pattern, t=PACK, u=2, v=2)[:, u],
                prod2[:].rearrange(pattern, t=PACK, u=2, v=2)[:, u],
                ALU.add,
            )

        def z_quantise(u):
            nc.vector.quantize_mx(out=z_codes[u][:].bitcast(FP8X4), scales=z_scales[u][:], in_=z_bf[u][:])

        def z2_product(n):
            cols = HALVES[n]
            z2_bf[n] = rounded_tile(f"z2_bf{n}", tag="z2_bf0" if n == 0 else "z_bf1")
            nc.vector.tensor_tensor(
                z2_bf[n][:].rearrange("p (c i t) -> p c t i", i=LINE, t=PACK),
                half_inv[:, PACK * cols.start : PACK * cols.stop].rearrange("p (t c i) -> p c t i", t=PACK, i=LINE),
                y_gb[:].rearrange("p (t c i) -> p c t i", t=PACK, i=LINE)[:, cols.start // LINE : cols.stop // LINE],
                ALU.mult,
            )

        def z2_quantise(n):
            cols = HALVES[n]
            nc.vector.quantize_mx(out=z2_codes[:, cols].bitcast(FP8X4), scales=z2_scales[:, cols], in_=z2_bf[n][:])

        def s_product(t, cols):
            u, v = divmod(t, 2)
            m_cols = slice(v * P, (v + 1) * P)
            nc.tensor.matmul_mx(
                out=s_ps[t][:, cols],
                lhsT=z_codes[u][:, m_cols].bitcast(FP8X4),
                lhsT_scale=z_scales[u][:, m_cols],
                rhs=z2_codes[:, cols].bitcast(FP8X4),
                rhs_scale=z2_scales[:, cols],
                start=True,
                stop=True,
            )

        def s_copy(t, cols):
            nc.scalar.activation(s[t][:, cols], s_ps[t][:, cols], ACT.Copy, scale=S_SCALE)

        z_sum(0)
        z2_product(0)
        z_quantise(0)
        z2_quantise(0)
        for t in (0, 1):
            s_product(t, HALVES[0])
            s_copy(t, HALVES[0])
        z2_product(1)
        z2_quantise(1)
        for t in (0, 1):
            s_product(t, HALVES[1])
        z_sum(1)
        z_quantise(1)
        for t in (2, 3):
            s_product(t, WHOLE)

        gate = sb.tile([P, PACK * S - S // 2], F32, name="gate")
        gate_first = (S // 2, 0, 3 * S // 2, 5 * S // 2)
        st = [sb.tile([P, 2 * S], F32, name=f"st{t}") for t in range(PACK)]
        st_n5 = sb.tile([P, PACK * S], F32, name="st_n5")
        res = sb.tile([P, PACK * S], F32, name="res")
        out_rows = out.rearrange("(p t) j -> p t j", t=PACK)

        def gate_and_st(t):
            s_copy(t, HALVES[1] if t < 2 else WHOLE)
            for cols in HALVES if t == 0 else (WHOLE,):
                gate_t = gate[:, gate_first[t] + cols.start : gate_first[t] + cols.stop]
                nc.scalar.activation(gate_t, look_up(s[t], n5_t, cols), ACT.Sigmoid)
                nc.vector.tensor_tensor(st[t][:, cols], s[t][:, cols], gate_t, ALU.mult)

        def fetch(t):
            for cols in HALVES if t == LAST else (WHOLE,):
                nc.vector.tensor_copy(st_n5[:, in_tile(t, cols)], look_up(st[t], n5_t, cols))

        def finish(t):
            for cols in HALVES if t == LAST else (WHOLE,):
                nc.vector.tensor_tensor(res[:, in_tile(t, cols)], st[t][:, cols], st_n5[:, in_tile(t, cols)], ALU.max)
                nc.sync.dma_start(out_rows[:, t, cols], res[:, in_tile(t, cols)])

        gate_and_st(0)
        fetch(0)
        for t in range(1, PACK):
            gate_and_st(t)
            finish(t - 1)
            fetch(t)
        finish(LAST)
